import numpy as np
import ml_dtypes


def mxq(x, axis, fmt="e4m3"):
    dtype, down = {"e4m3": (ml_dtypes.float8_e4m3fn, 7), "e5m2": (ml_dtypes.float8_e5m2, 14)}[fmt]
    v = np.moveaxis(np.asarray(x, np.float32).astype(ml_dtypes.bfloat16).astype(np.float64), axis, -1)
    blocks = v.reshape(v.shape[:-1] + (-1, 32))
    amax = np.abs(blocks).max(-1, keepdims=True)
    byte = np.maximum(np.where(amax > 0, np.frexp(amax)[1] - 1 + 127, 0) - down, 1)
    scale = np.exp2(byte - 127.0)
    codes = (blocks / scale).astype(np.float32).astype(dtype).astype(np.float64)
    return np.moveaxis((codes * scale).reshape(v.shape), -1, axis)


WIDE = False


def mx_kscale(k):
    if not WIDE:
        return np.ones(k)
    levels = np.array([30, -30])
    if k % 512:
        return np.exp2(np.random.permutation(np.resize(levels, k // 32))).repeat(32)
    a = np.empty((k // 512, 16))
    for p in range(k // 512):
        a[p, :8] = np.random.permutation(np.resize(levels, 8))
        for g in range(8):
            far = levels[np.abs(levels - a[p, g]) >= 10]
            a[p, g + 8] = far[np.random.randint(len(far))]
    return np.exp2(a.ravel()).repeat(32)


def f64(x):
    return np.asarray(x).astype(np.float64)


def striped(idx):
    return np.tile(np.asarray(idx).reshape(-1, 16).T, (8, 1)).astype(np.uint16)


def unstriped(offs):
    return offs[:16].T.reshape(-1).astype(np.int64)


E2M1 = np.array([0.0, 0.5, 1.0, 1.5, 2.0, 3.0, 4.0, 6.0, -0.0, -0.5, -1.0, -1.5, -2.0, -3.0, -4.0, -6.0])


def pack_weight(w, fmt):
    k, n = w.shape
    w = f64(np.asarray(w, np.float32).astype(ml_dtypes.bfloat16)).reshape(k // 32, 32, n)
    amax = np.abs(w).max(1)
    if fmt in ("e4m3", "e5m2"):
        byte = np.frexp(amax)[1] - 1 + 127 - (7 if fmt == "e4m3" else 14)
    else:
        mant, ex = np.frexp(amax / 6.0)
        byte = np.where(mant > 0.5, ex, ex - 1) + 127
    byte = np.clip(np.where(amax > 0, byte, 1), 1, 254)
    scaled = (w * np.exp2(127.0 - byte)[:, None, :]).reshape(k, n).astype(np.float32)
    by_word = np.ascontiguousarray(scaled.reshape(k // 512, 128, 4, n).transpose(0, 1, 3, 2))
    if fmt in ("e4m3", "e5m2"):
        words = by_word.astype(ml_dtypes.float8_e4m3fn if fmt == "e4m3" else ml_dtypes.float8_e5m2).view(np.uint8)
    else:
        c = by_word.astype(ml_dtypes.float4_e2m1fn).view(np.uint8) & 0xF
        words = (c[..., 0::2] | (c[..., 1::2] << 4)).reshape(k // 512, 128, 2 * n)
    return np.ascontiguousarray(words), np.ascontiguousarray(byte.astype(np.uint8).reshape(k // 512, 16, n))


def unpack_weight(words, scales, fmt):
    g, _, n = scales.shape
    words = np.ascontiguousarray(words).reshape(g, 128, n, -1)
    if fmt in ("e4m3", "e5m2"):
        vals = words.view(ml_dtypes.float8_e4m3fn if fmt == "e4m3" else ml_dtypes.float8_e5m2).astype(np.float64)
    else:
        nib = np.empty((g, 128, n, 4), np.uint8)
        nib[..., 0::2] = words & 0xF
        nib[..., 1::2] = words >> 4
        vals = E2M1[nib]
    vals = vals * np.repeat(np.exp2(scales.astype(np.float64) - 127.0), 8, axis=1)[..., None]
    return vals.transpose(0, 1, 3, 2).reshape(g * 512, n)


K, T, Z, J, R, C, I, O, N = 512, 1024, 1024, 256, 512, 512, 128, 128, 256


def setup_inputs():
    n = np.random.standard_normal
    idx = np.random.permutation(T)[:J]
    idx2 = np.random.permutation(Z)[:J]
    idx3 = np.random.permutation(J)[:I]
    idx4 = np.random.permutation(C)[:I]
    idx5 = np.random.permutation(C)[:O]
    idx6 = np.random.permutation(J)[:O]
    idx7 = np.random.permutation(T)[:O]
    fk = mx_kscale(K)
    fr = mx_kscale(R)
    xtp = pack_weight(n((K, T)) / fk[:, None], "e4m3")
    xop = pack_weight(n((K, Z)) / fk[:, None], "e2m1")
    wp = pack_weight(n((K, R)) * 1 / np.sqrt(K) * fk[:, None] * fr, "e5m2")
    wbp = pack_weight(n((R, N)) * 1 / np.sqrt(R) / fr[:, None], "e5m2")
    wsp = pack_weight(n((K, N)) * 1 / np.sqrt(K) * fk[:, None], "e5m2")
    return {
        "xt_words": xtp[0],
        "xt_scales": xtp[1],
        "xo_words": xop[0],
        "xo_scales": xop[1],
        "w_words": wp[0],
        "w_scales": wp[1],
        "sa": (np.random.uniform(0.5, 1.6, (R, 1))).astype(np.float32),
        "wb_words": wbp[0],
        "wb_scales": wbp[1],
        "ws_words": wsp[0],
        "ws_scales": wsp[1],
        "offs": striped(idx),
        "offs2": striped(idx2),
        "offs3": striped(idx3),
        "offs4": striped(idx4),
        "offs5": striped(idx5),
        "offs6": striped(idx6),
        "offs7": striped(idx7),
    }


def reference(xt_words, xt_scales, xo_words, xo_scales, w_words, w_scales, sa, wb_words, wb_scales, ws_words, ws_scales, offs, offs2, offs3, offs4, offs5, offs6, offs7):
    idx = unstriped(offs)
    idx2 = unstriped(offs2)
    idx3 = unstriped(offs3)
    idx4 = unstriped(offs4)
    idx5 = unstriped(offs5)
    idx6 = unstriped(offs6)
    idx7 = unstriped(offs7)
    xtu = unpack_weight(xt_words, xt_scales, "e4m3")
    xou = unpack_weight(xo_words, xo_scales, "e2m1")
    wu = unpack_weight(w_words, w_scales, "e5m2")
    wbu = unpack_weight(wb_words, wb_scales, "e5m2")
    wsu = unpack_weight(ws_words, ws_scales, "e5m2")
    xtidxg = xtu[:, idx]
    a = wu.T @ xtidxg
    xoidx2g = xou[:, idx2]
    b = wu.T @ xoidx2g
    h1 = a[:, idx3] * f64(sa)
    pw = np.zeros((R, C))
    pw[:, idx4] = h1
    hid = np.maximum(pw[:, idx5], b[:, idx6])
    hidq = mxq(hid, 0, "e4m3")
    xtidx7g = xtu[:, idx7]
    y = wbu.T @ hidq + wsu.T @ xtidx7g
    return y

@@ -1,0 +1,181 @@
+from contextlib import ExitStack
+
+import concourse.mybir as mybir
+
+K, T, Z, J, R, C, I, O, N = 512, 1024, 1024, 256, 512, 512, 128, 128, 256
+FLOPS = 2 * (2 * K * R * J + R * N * O + K * N * O)
+
+F32 = mybir.dt.float32
+BF16 = mybir.dt.bfloat16
+I32 = mybir.dt.int32
+U32 = mybir.dt.uint32
+U16 = mybir.dt.uint16
+U8 = mybir.dt.uint8
+E4M3 = mybir.dt.float8_e4m3fn_x4
+E5M2 = mybir.dt.float8_e5m2_x4
+E2M1 = mybir.dt.float4_e2m1fn_x4
+COPY = mybir.ActivationFunctionType.Copy
+MAX = mybir.AluOpType.max
+
+P = 128
+PACK = 4
+
+
+def tile_list_weighedposting_oneforboth_further_plain_kernel(
+    tc, xt_words, xt_scales, xo_words, xo_scales, w_words, w_scales, sa, wb_words, wb_scales,
+    ws_words, ws_scales, offs, offs2, offs3, offs4, offs5, offs6, offs7, out,
+):
+    nc = tc.nc
+    with ExitStack() as ctx:
+        sb = ctx.enter_context(tc.tile_pool(name="sb", bufs=1))
+        ps = ctx.enter_context(tc.psum_pool(name="ps", bufs=1))
+
+        def tile(shape, dtype, name):
+            return sb.tile(shape, dtype, name=name, align_bytes=64)
+
+        def load_list(src, name):
+            lst = tile([P, src.shape[1]], U16, name)
+            nc.sync.dma_start(lst[:], src)
+            return lst
+
+        def load_words(src, width, dtype, name):
+            words = tile([P, width], dtype, name)
+            nc.sync.dma_start(words[:].bitcast(I32), src.bitcast(I32))
+            return words
+
+        def zeroed_plane(width, name):
+            plane = tile([P, width], U8, name)
+            nc.vector.memset(plane[:].bitcast(I32), 0)
+            return plane
+
+        def load_plane(queue, plane, scales):
+            for q in range(4):
+                queue.dma_start(
+                    plane[32 * q : 32 * q + 4, :].bitcast(I32), scales[0, 4 * q : 4 * q + 4, :].bitcast(I32)
+                )
+
+        def flat(words):
+            return words[0].rearrange("p n t -> p (n t)")
+
+        xt_plane = zeroed_plane(T, "xt_plane")
+        w_plane = zeroed_plane(R, "w_plane")
+        xo_plane = zeroed_plane(Z, "xo_plane")
+        out_planes = zeroed_plane(2 * N, "out_planes")
+        board = [tile([P, C], F32, "board%d" % t) for t in range(PACK)]
+        for t in range(PACK):
+            nc.vector.memset(board[t][:], 0.0)
+
+        idx = load_list(offs, "idx")
+        w_rows = tile([4, 4, R], U8, "w_rows")
+        nc.sync.dma_start(
+            w_rows[:].bitcast(I32), w_scales[0].bitcast(I32).rearrange("(q r) n -> r q n", r=4)
+        )
+        w_raw = load_words(flat(w_words), R, U32, "w_raw")
+        load_plane(nc.scalar, xt_plane, xt_scales)
+        xt_w = load_words(flat(xt_words), T, U32, "xt_w")
+        idx3 = load_list(offs3, "idx3")
+        sa_sb = tile([P, PACK], F32, "sa_sb")
+        nc.sync.dma_start(sa_sb[:], sa.rearrange("(p t) one -> p (t one)", t=PACK))
+        idx2 = load_list(offs2, "idx2")
+        xo_w = load_words(xo_words[0], Z, U16, "xo_w")
+        load_plane(nc.sync, xo_plane, xo_scales)
+        idx4 = load_list(offs4, "idx4")
+        idx7 = load_list(offs7, "idx7")
+        idx5 = load_list(offs5, "idx5")
+        idx6 = load_list(offs6, "idx6")
+        ws_w = load_words(flat(ws_words), N, U32, "ws_w")
+        wb_w = load_words(flat(wb_words), N, U32, "wb_w")
+        load_plane(nc.sync, out_planes[:, 0:N], ws_scales)
+        load_plane(nc.sync, out_planes[:, N : 2 * N], wb_scales)
+
+        for q in range(4):
+            nc.vector.tensor_copy(w_plane[32 * q : 32 * q + 4, :].bitcast(I32), w_rows[:, q, :].bitcast(I32))
+        w_sc = tile([P, R], U8, "w_sc")
+        nc.vector.tensor_copy(
+            w_sc[:].rearrange("p (t c i) -> p c t i", t=PACK, i=16),
+            w_plane[:].rearrange("p (c i t) -> p c t i", t=PACK, i=16),
+        )
+        w_w = tile([P, R], U32, "w_w")
+        nc.scalar.copy(
+            w_w[:].rearrange("p (t c i) -> p c t i", t=PACK, i=4),
+            w_raw[:].rearrange("p (c i t) -> p c t i", t=PACK, i=4),
+        )
+
+        def gather_packed(words, plane, lst, count, dtype, name):
+            g_s = tile([P, count], U8, name + "_s")
+            nc.vector.tensor_copy(g_s[:], plane[:].indirect(lst[:]))
+            g_w = tile([P, count], dtype, name + "_w")
+            nc.vector.tensor_copy(g_w[:], words[:].indirect(lst[:]))
+            return g_w, g_s
+
+        def first_stage(acc, t, g_w, g_s, fmt):
+            cols = slice(t * P, (t + 1) * P)
+            nc.tensor.matmul_mx(
+                out=acc, lhsT=w_w[:, cols].bitcast(E5M2), lhsT_scale=w_sc[:, cols],
+                rhs=g_w[:].bitcast(fmt), rhs_scale=g_s[:], start=True, stop=True,
+            )
+
+        xg_w, xg_s = gather_packed(xt_w, xt_plane, idx, J, U32, "xg")
+        a_ps = [ps.tile([P, J], F32, name="a_ps%d" % t) for t in range(PACK)]
+        for t in range(PACK):
+            first_stage(a_ps[t][:], t, xg_w, xg_s, E4M3)
+
+        og_w, og_s = gather_packed(xo_w, xo_plane, idx2, J, U16, "og")
+        b_ps = [ps.tile([P, 2, J], F32, name="b_ps%d" % u) for u in range(2)]
+        for t in range(PACK):
+            first_stage(b_ps[t // 2][:, t % 2, :], t, og_w, og_s, E2M1)
+
+        x7_w, x7_s = gather_packed(xt_w, xt_plane, idx7, O, U32, "x7")
+        y_ps = [ps.tile([P, O], F32, name="y_ps%d" % m) for m in range(2)]
+        for m in range(2):
+            nc.tensor.matmul_mx(
+                out=y_ps[m][:], lhsT=ws_w[:, m * P : (m + 1) * P].bitcast(E5M2),
+                lhsT_scale=out_planes[:, m * P : (m + 1) * P],
+                rhs=x7_w[:].bitcast(E4M3), rhs_scale=x7_s[:], start=True, stop=False,
+            )
+
+        a_sb = [tile([P, J], F32, "a_sb%d" % t) for t in range(PACK)]
+        h1 = [tile([P, I], F32, "h1_%d" % t) for t in range(PACK)]
+        for pair in range(2):
+            for t in (2 * pair, 2 * pair + 1):
+                nc.scalar.copy(a_sb[t][:], a_ps[t][:])
+            for t in (2 * pair, 2 * pair + 1):
+                nc.scalar.activation(h1[t][:], a_sb[t][:].indirect(idx3[:]), COPY, scale=sa_sb[:, t : t + 1])
+
+        b_sb = [tile([P, J], F32, "b_sb%d" % t) for t in range(PACK)]
+        for t in range(PACK):
+            nc.scalar.copy(b_sb[t][:], b_ps[t // 2][:, t % 2, :])
+
+        for t in range(PACK - 1):
+            nc.vector.tensor_copy(board[t][:].indirect(idx4[:]), h1[t][:])
+        nc.scalar.activation(board[3][:].indirect(idx4[:]), h1[3][:], COPY)
+
+        pg = tile([P, PACK, O], F32, "pg")
+        bg = tile([P, PACK, O], F32, "bg")
+        for t in range(PACK):
+            nc.vector.tensor_copy(pg[:, t, :], board[t][:].indirect(idx5[:]))
+        for t in range(PACK):
+            nc.scalar.activation(bg[:, t, :], b_sb[t][:].indirect(idx6[:]), COPY)
+
+        hid = tile([P, O, PACK], BF16, "hid")
+        nc.vector.tensor_tensor(
+            hid[:].rearrange("p (c i) t -> p c t i", i=4),
+            pg[:].rearrange("p t (c i) -> p c t i", i=4),
+            bg[:].rearrange("p t (c i) -> p c t i", i=4),
+            MAX,
+        )
+        hid_w = tile([P, O], U32, "hid_w")
+        hid_s = tile([P, O], U8, "hid_s")
+        nc.vector.quantize_mx(out=hid_w[:].bitcast(E4M3), scales=hid_s[:], in_=hid[:].rearrange("p o t -> p (o t)"))
+
+        y_sb = [tile([P, O], F32, "y_sb%d" % m) for m in range(2)]
+        for m in range(2):
+            nc.tensor.matmul_mx(
+                out=y_ps[m][:], lhsT=wb_w[:, m * P : (m + 1) * P].bitcast(E5M2),
+                lhsT_scale=out_planes[:, N + m * P : N + (m + 1) * P],
+                rhs=hid_w[:].bitcast(E4M3), rhs_scale=hid_s[:], start=False, stop=True,
+            )
+        nc.scalar.copy(y_sb[0][:], y_ps[0][:])
+        nc.scalar.dma_start(out[0:P, :], y_sb[0][:])
+        nc.vector.tensor_copy(y_sb[1][:], y_ps[1][:])
+        nc.sync.dma_start(out[P : 2 * P, :], y_sb[1][:])

@@ -38,9 +38,9 @@ def tile_list_weighedposting_oneforboth_further_plain_kernel(
             nc.sync.dma_start(lst[:], src)
             return lst
 
-        def load_words(src, width, dtype, name):
+        def load_words(queue, src, width, dtype, name):
             words = tile([P, width], dtype, name)
-            nc.sync.dma_start(words[:].bitcast(I32), src.bitcast(I32))
+            queue.dma_start(words[:].bitcast(I32), src.bitcast(I32))
             return words
 
         def zeroed_plane(width, name):
@@ -57,43 +57,41 @@ def tile_list_weighedposting_oneforboth_further_plain_kernel(
         def flat(words):
             return words[0].rearrange("p n t -> p (n t)")
 
+        w_plane = tile([P, 2 * R], U8, "w_plane")
+        nc.gpsimd.memset(w_plane[0:64, :].bitcast(I32), 0)
         xt_plane = zeroed_plane(T, "xt_plane")
-        w_plane = zeroed_plane(R, "w_plane")
         xo_plane = zeroed_plane(Z, "xo_plane")
         out_planes = zeroed_plane(2 * N, "out_planes")
-        board = [tile([P, C], F32, "board%d" % t) for t in range(PACK)]
-        for t in range(PACK):
-            nc.vector.memset(board[t][:], 0.0)
 
         idx = load_list(offs, "idx")
-        w_rows = tile([4, 4, R], U8, "w_rows")
-        nc.sync.dma_start(
-            w_rows[:].bitcast(I32), w_scales[0].bitcast(I32).rearrange("(q r) n -> r q n", r=4)
-        )
-        w_raw = load_words(flat(w_words), R, U32, "w_raw")
-        load_plane(nc.scalar, xt_plane, xt_scales)
-        xt_w = load_words(flat(xt_words), T, U32, "xt_w")
         idx3 = load_list(offs3, "idx3")
         sa_sb = tile([P, PACK], F32, "sa_sb")
         nc.sync.dma_start(sa_sb[:], sa.rearrange("(p t) one -> p (t one)", t=PACK))
+        w_raw = load_words(nc.sync, flat(w_words), R, U32, "w_raw")
+        w_rows = w_scales[0].bitcast(I32).rearrange("(h g r) n -> g r h n", h=2, g=2)
+        for g in range(2):
+            nc.sync.dma_start(
+                w_plane[32 * g : 32 * g + 4, :].bitcast(I32).rearrange("r (h n) -> r h n", h=2), w_rows[g]
+            )
+        xt_w = load_words(nc.sync, flat(xt_words), T, U32, "xt_w")
+        load_plane(nc.sync, xt_plane, xt_scales)
+        idx7 = load_list(offs7, "idx7")
+        xo_w = load_words(nc.sync, xo_words[0], Z, U16, "xo_w")
         idx2 = load_list(offs2, "idx2")
-        xo_w = load_words(xo_words[0], Z, U16, "xo_w")
         load_plane(nc.sync, xo_plane, xo_scales)
         idx4 = load_list(offs4, "idx4")
-        idx7 = load_list(offs7, "idx7")
         idx5 = load_list(offs5, "idx5")
         idx6 = load_list(offs6, "idx6")
-        ws_w = load_words(flat(ws_words), N, U32, "ws_w")
-        wb_w = load_words(flat(wb_words), N, U32, "wb_w")
+        ws_w = load_words(nc.sync, flat(ws_words), N, U32, "ws_w")
+        wb_w = load_words(nc.sync, flat(wb_words), N, U32, "wb_w")
         load_plane(nc.sync, out_planes[:, 0:N], ws_scales)
         load_plane(nc.sync, out_planes[:, N : 2 * N], wb_scales)
 
-        for q in range(4):
-            nc.vector.tensor_copy(w_plane[32 * q : 32 * q + 4, :].bitcast(I32), w_rows[:, q, :].bitcast(I32))
+        nc.vector.tensor_copy(w_plane[64:128, 0:R].bitcast(I32), w_plane[0:64, R : 2 * R].bitcast(I32))
         w_sc = tile([P, R], U8, "w_sc")
         nc.vector.tensor_copy(
             w_sc[:].rearrange("p (t c i) -> p c t i", t=PACK, i=16),
-            w_plane[:].rearrange("p (c i t) -> p c t i", t=PACK, i=16),
+            w_plane[:, 0:R].rearrange("p (c i t) -> p c t i", t=PACK, i=16),
         )
         w_w = tile([P, R], U32, "w_w")
         nc.scalar.copy(
@@ -102,10 +100,10 @@ def tile_list_weighedposting_oneforboth_further_plain_kernel(
         )
 
         def gather_packed(words, plane, lst, count, dtype, name):
-            g_s = tile([P, count], U8, name + "_s")
-            nc.vector.tensor_copy(g_s[:], plane[:].indirect(lst[:]))
             g_w = tile([P, count], dtype, name + "_w")
             nc.vector.tensor_copy(g_w[:], words[:].indirect(lst[:]))
+            g_s = tile([P, count], U8, name + "_s")
+            nc.vector.tensor_copy(g_s[:], plane[:].indirect(lst[:]))
             return g_w, g_s
 
         def first_stage(acc, t, g_w, g_s, fmt):
@@ -120,12 +118,12 @@ def tile_list_weighedposting_oneforboth_further_plain_kernel(
         for t in range(PACK):
             first_stage(a_ps[t][:], t, xg_w, xg_s, E4M3)
 
+        x7_w, x7_s = gather_packed(xt_w, xt_plane, idx7, O, U32, "x7")
         og_w, og_s = gather_packed(xo_w, xo_plane, idx2, J, U16, "og")
         b_ps = [ps.tile([P, 2, J], F32, name="b_ps%d" % u) for u in range(2)]
         for t in range(PACK):
             first_stage(b_ps[t // 2][:, t % 2, :], t, og_w, og_s, E2M1)
 
-        x7_w, x7_s = gather_packed(xt_w, xt_plane, idx7, O, U32, "x7")
         y_ps = [ps.tile([P, O], F32, name="y_ps%d" % m) for m in range(2)]
         for m in range(2):
             nc.tensor.matmul_mx(
@@ -142,13 +140,16 @@ def tile_list_weighedposting_oneforboth_further_plain_kernel(
             for t in (2 * pair, 2 * pair + 1):
                 nc.scalar.activation(h1[t][:], a_sb[t][:].indirect(idx3[:]), COPY, scale=sa_sb[:, t : t + 1])
 
+        board = [tile([P, C], F32, "board%d" % t) for t in range(PACK)]
+        for t in range(PACK):
+            nc.gpsimd.memset(board[t][:], 0.0)
+        for t in (0, 1, 3):
+            nc.vector.tensor_copy(board[t][:].indirect(idx4[:]), h1[t][:])
+        nc.scalar.activation(board[2][:].indirect(idx4[:]), h1[2][:], COPY)
+
         b_sb = [tile([P, J], F32, "b_sb%d" % t) for t in range(PACK)]
         for t in range(PACK):
             nc.scalar.copy(b_sb[t][:], b_ps[t // 2][:, t % 2, :])
-
-        for t in range(PACK - 1):
-            nc.vector.tensor_copy(board[t][:].indirect(idx4[:]), h1[t][:])
-        nc.scalar.activation(board[3][:].indirect(idx4[:]), h1[3][:], COPY)
 
         pg = tile([P, PACK, O], F32, "pg")
         bg = tile([P, PACK, O], F32, "bg")
@@ -158,15 +159,20 @@ def tile_list_weighedposting_oneforboth_further_plain_kernel(
             nc.scalar.activation(bg[:, t, :], b_sb[t][:].indirect(idx6[:]), COPY)
 
         hid = tile([P, O, PACK], BF16, "hid")
-        nc.vector.tensor_tensor(
-            hid[:].rearrange("p (c i) t -> p c t i", i=4),
-            pg[:].rearrange("p t (c i) -> p c t i", i=4),
-            bg[:].rearrange("p t (c i) -> p c t i", i=4),
-            MAX,
-        )
         hid_w = tile([P, O], U32, "hid_w")
         hid_s = tile([P, O], U8, "hid_s")
-        nc.vector.quantize_mx(out=hid_w[:].bitcast(E4M3), scales=hid_s[:], in_=hid[:].rearrange("p o t -> p (o t)"))
+        halves = [slice(0, O // 2), slice(O // 2, O)]
+        for h in halves:
+            nc.vector.tensor_tensor(
+                hid[:, h, :].rearrange("p (c i) t -> p c t i", i=4),
+                pg[:, :, h].rearrange("p t (c i) -> p c t i", i=4),
+                bg[:, :, h].rearrange("p t (c i) -> p c t i", i=4),
+                MAX,
+            )
+        for h in halves:
+            nc.vector.quantize_mx(
+                out=hid_w[:, h].bitcast(E4M3), scales=hid_s[:, h], in_=hid[:, h, :].rearrange("p o t -> p (o t)")
+            )
 
         y_sb = [tile([P, O], F32, "y_sb%d" % m) for m in range(2)]
         for m in range(2):

@@ -63,21 +63,18 @@ def tile_list_weighedposting_oneforboth_further_plain_kernel(
         xo_plane = zeroed_plane(Z, "xo_plane")
         out_planes = zeroed_plane(2 * N, "out_planes")
 
+        w_rows = tile([4, 4, R], U8, "w_rows")
+        nc.sync.dma_start(w_rows[:].bitcast(I32), w_scales[0].bitcast(I32).rearrange("(q r) n -> r q n", r=4))
+        xt_w = load_words(nc.sync, flat(xt_words), T, U32, "xt_w")
         idx = load_list(offs, "idx")
+        w_raw = load_words(nc.sync, flat(w_words), R, U32, "w_raw")
+        load_plane(nc.sync, xt_plane, xt_scales)
+        idx7 = load_list(offs7, "idx7")
+        idx2 = load_list(offs2, "idx2")
+        xo_w = load_words(nc.sync, xo_words[0], Z, U16, "xo_w")
         idx3 = load_list(offs3, "idx3")
         sa_sb = tile([P, PACK], F32, "sa_sb")
         nc.sync.dma_start(sa_sb[:], sa.rearrange("(p t) one -> p (t one)", t=PACK))
-        w_raw = load_words(nc.sync, flat(w_words), R, U32, "w_raw")
-        w_rows = w_scales[0].bitcast(I32).rearrange("(h g r) n -> g r h n", h=2, g=2)
-        for g in range(2):
-            nc.sync.dma_start(
-                w_plane[32 * g : 32 * g + 4, :].bitcast(I32).rearrange("r (h n) -> r h n", h=2), w_rows[g]
-            )
-        xt_w = load_words(nc.sync, flat(xt_words), T, U32, "xt_w")
-        load_plane(nc.sync, xt_plane, xt_scales)
-        idx7 = load_list(offs7, "idx7")
-        xo_w = load_words(nc.sync, xo_words[0], Z, U16, "xo_w")
-        idx2 = load_list(offs2, "idx2")
         load_plane(nc.sync, xo_plane, xo_scales)
         idx4 = load_list(offs4, "idx4")
         idx5 = load_list(offs5, "idx5")
@@ -87,6 +84,11 @@ def tile_list_weighedposting_oneforboth_further_plain_kernel(
         load_plane(nc.sync, out_planes[:, 0:N], ws_scales)
         load_plane(nc.sync, out_planes[:, N : 2 * N], wb_scales)
 
+        for g in range(2):
+            nc.vector.tensor_copy(
+                w_plane[32 * g : 32 * g + 4, :].bitcast(I32).rearrange("r (h n) -> r h n", h=2),
+                w_rows[:].bitcast(I32).rearrange("r (h g) n -> r g h n", g=2)[:, g, :, :],
+            )
         nc.vector.tensor_copy(w_plane[64:128, 0:R].bitcast(I32), w_plane[0:64, R : 2 * R].bitcast(I32))
         w_sc = tile([P, R], U8, "w_sc")
         nc.vector.tensor_copy(
@@ -119,6 +121,20 @@ def tile_list_weighedposting_oneforboth_further_plain_kernel(
             first_stage(a_ps[t][:], t, xg_w, xg_s, E4M3)
 
         x7_w, x7_s = gather_packed(xt_w, xt_plane, idx7, O, U32, "x7")
+        a_sb = [tile([P, J], F32, "a_sb%d" % t) for t in range(PACK)]
+        h1 = [tile([P, I], F32, "h1_%d" % t) for t in range(PACK)]
+
+        def weigh(t):
+            nc.scalar.activation(h1[t][:], a_sb[t][:].indirect(idx3[:]), COPY, scale=sa_sb[:, t : t + 1])
+
+        nc.scalar.copy(a_sb[0][:], a_ps[0][:])
+        nc.vector.tensor_copy(a_sb[1][:], a_ps[1][:])
+        weigh(0)
+        nc.scalar.copy(a_sb[2][:], a_ps[2][:])
+        nc.scalar.copy(a_sb[3][:], a_ps[3][:])
+        for t in (2, 3, 1):
+            weigh(t)
+
         og_w, og_s = gather_packed(xo_w, xo_plane, idx2, J, U16, "og")
         b_ps = [ps.tile([P, 2, J], F32, name="b_ps%d" % u) for u in range(2)]
         for t in range(PACK):
@@ -132,20 +148,12 @@ def tile_list_weighedposting_oneforboth_further_plain_kernel(
                 rhs=x7_w[:].bitcast(E4M3), rhs_scale=x7_s[:], start=True, stop=False,
             )
 
-        a_sb = [tile([P, J], F32, "a_sb%d" % t) for t in range(PACK)]
-        h1 = [tile([P, I], F32, "h1_%d" % t) for t in range(PACK)]
-        for pair in range(2):
-            for t in (2 * pair, 2 * pair + 1):
-                nc.scalar.copy(a_sb[t][:], a_ps[t][:])
-            for t in (2 * pair, 2 * pair + 1):
-                nc.scalar.activation(h1[t][:], a_sb[t][:].indirect(idx3[:]), COPY, scale=sa_sb[:, t : t + 1])
-
         board = [tile([P, C], F32, "board%d" % t) for t in range(PACK)]
         for t in range(PACK):
-            nc.gpsimd.memset(board[t][:], 0.0)
-        for t in (0, 1, 3):
+            (nc.gpsimd if t < 2 else nc.vector).memset(board[t][:], 0.0)
+        for t in (0, 2, 1):
             nc.vector.tensor_copy(board[t][:].indirect(idx4[:]), h1[t][:])
-        nc.scalar.activation(board[2][:].indirect(idx4[:]), h1[2][:], COPY)
+        nc.scalar.activation(board[3][:].indirect(idx4[:]), h1[3][:], COPY)
 
         b_sb = [tile([P, J], F32, "b_sb%d" % t) for t in range(PACK)]
         for t in range(PACK):
@@ -153,7 +161,7 @@ def tile_list_weighedposting_oneforboth_further_plain_kernel(
 
         pg = tile([P, PACK, O], F32, "pg")
         bg = tile([P, PACK, O], F32, "bg")
-        for t in range(PACK):
+        for t in (0, 2, 1, 3):
             nc.vector.tensor_copy(pg[:, t, :], board[t][:].indirect(idx5[:]))
         for t in range(PACK):
             nc.scalar.activation(bg[:, t, :], b_sb[t][:].indirect(idx6[:]), COPY)

from contextlib import ExitStack

import concourse.mybir as mybir

K, T, Z, J, R, C, I, O, N = 512, 1024, 1024, 256, 512, 512, 128, 128, 256
FLOPS = 2 * (2 * K * R * J + R * N * O + K * N * O)

F32 = mybir.dt.float32
BF16 = mybir.dt.bfloat16
I32 = mybir.dt.int32
U32 = mybir.dt.uint32
U16 = mybir.dt.uint16
U8 = mybir.dt.uint8
E4M3 = mybir.dt.float8_e4m3fn_x4
E5M2 = mybir.dt.float8_e5m2_x4
E2M1 = mybir.dt.float4_e2m1fn_x4
COPY = mybir.ActivationFunctionType.Copy
MAX = mybir.AluOpType.max

P = 128
PACK = 4


def tile_list_weighedposting_oneforboth_further_plain_kernel(
    tc, xt_words, xt_scales, xo_words, xo_scales, w_words, w_scales, sa, wb_words, wb_scales,
    ws_words, ws_scales, offs, offs2, offs3, offs4, offs5, offs6, offs7, out,
):
    nc = tc.nc
    with ExitStack() as ctx:
        sb = ctx.enter_context(tc.tile_pool(name="sb", bufs=1))
        ps = ctx.enter_context(tc.psum_pool(name="ps", bufs=1))

        def tile(shape, dtype, name):
            return sb.tile(shape, dtype, name=name, align_bytes=64)

        def load_list(src, name):
            lst = tile([P, src.shape[1]], U16, name)
            nc.sync.dma_start(lst[:], src)
            return lst

        def load_words(queue, src, width, dtype, name):
            words = tile([P, width], dtype, name)
            queue.dma_start(words[:].bitcast(I32), src.bitcast(I32))
            return words

        def zeroed_plane(width, name):
            plane = tile([P, width], U8, name)
            nc.vector.memset(plane[:].bitcast(I32), 0)
            return plane

        def load_plane(queue, plane, scales):
            for q in range(4):
                queue.dma_start(
                    plane[32 * q : 32 * q + 4, :].bitcast(I32), scales[0, 4 * q : 4 * q + 4, :].bitcast(I32)
                )

        def flat(words):
            return words[0].rearrange("p n t -> p (n t)")

        w_plane = tile([P, 2 * R], U8, "w_plane")
        nc.gpsimd.memset(w_plane[0:64, :].bitcast(I32), 0)
        xt_plane = zeroed_plane(T, "xt_plane")
        xo_plane = zeroed_plane(Z, "xo_plane")
        out_planes = zeroed_plane(2 * N, "out_planes")

        w_rows = tile([4, 4, R], U8, "w_rows")
        nc.sync.dma_start(w_rows[:].bitcast(I32), w_scales[0].bitcast(I32).rearrange("(q r) n -> r q n", r=4))
        xt_w = load_words(nc.sync, flat(xt_words), T, U32, "xt_w")
        idx = load_list(offs, "idx")
        w_raw = load_words(nc.sync, flat(w_words), R, U32, "w_raw")
        load_plane(nc.sync, xt_plane, xt_scales)
        idx7 = load_list(offs7, "idx7")
        idx2 = load_list(offs2, "idx2")
        xo_w = load_words(nc.sync, xo_words[0], Z, U16, "xo_w")
        idx3 = load_list(offs3, "idx3")
        sa_sb = tile([P, PACK], F32, "sa_sb")
        nc.sync.dma_start(sa_sb[:], sa.rearrange("(p t) one -> p (t one)", t=PACK))
        load_plane(nc.sync, xo_plane, xo_scales)
        idx4 = load_list(offs4, "idx4")
        idx5 = load_list(offs5, "idx5")
        idx6 = load_list(offs6, "idx6")
        ws_w = load_words(nc.sync, flat(ws_words), N, U32, "ws_w")
        wb_w = load_words(nc.sync, flat(wb_words), N, U32, "wb_w")
        load_plane(nc.sync, out_planes[:, 0:N], ws_scales)
        load_plane(nc.sync, out_planes[:, N : 2 * N], wb_scales)

        for g in range(2):
            nc.vector.tensor_copy(
                w_plane[32 * g : 32 * g + 4, :].bitcast(I32).rearrange("r (h n) -> r h n", h=2),
                w_rows[:].bitcast(I32).rearrange("r (h g) n -> r g h n", g=2)[:, g, :, :],
            )
        nc.vector.tensor_copy(w_plane[64:128, 0:R].bitcast(I32), w_plane[0:64, R : 2 * R].bitcast(I32))
        w_sc = tile([P, R], U8, "w_sc")
        nc.vector.tensor_copy(
            w_sc[:].rearrange("p (t c i) -> p c t i", t=PACK, i=16),
            w_plane[:, 0:R].rearrange("p (c i t) -> p c t i", t=PACK, i=16),
        )
        w_w = tile([P, R], U32, "w_w")
        nc.scalar.copy(
            w_w[:].rearrange("p (t c i) -> p c t i", t=PACK, i=4),
            w_raw[:].rearrange("p (c i t) -> p c t i", t=PACK, i=4),
        )

        def gather_packed(words, plane, lst, count, dtype, name):
            g_w = tile([P, count], dtype, name + "_w")
            nc.vector.tensor_copy(g_w[:], words[:].indirect(lst[:]))
            g_s = tile([P, count], U8, name + "_s")
            nc.vector.tensor_copy(g_s[:], plane[:].indirect(lst[:]))
            return g_w, g_s

        def first_stage(acc, t, g_w, g_s, fmt):
            cols = slice(t * P, (t + 1) * P)
            nc.tensor.matmul_mx(
                out=acc, lhsT=w_w[:, cols].bitcast(E5M2), lhsT_scale=w_sc[:, cols],
                rhs=g_w[:].bitcast(fmt), rhs_scale=g_s[:], start=True, stop=True,
            )

        xg_w, xg_s = gather_packed(xt_w, xt_plane, idx, J, U32, "xg")
        a_ps = [ps.tile([P, J], F32, name="a_ps%d" % t) for t in range(PACK)]
        for t in range(PACK):
            first_stage(a_ps[t][:], t, xg_w, xg_s, E4M3)

        x7_w, x7_s = gather_packed(xt_w, xt_plane, idx7, O, U32, "x7")
        a_sb = [tile([P, J], F32, "a_sb%d" % t) for t in range(PACK)]
        h1 = [tile([P, I], F32, "h1_%d" % t) for t in range(PACK)]

        def weigh(t):
            nc.scalar.activation(h1[t][:], a_sb[t][:].indirect(idx3[:]), COPY, scale=sa_sb[:, t : t + 1])

        nc.scalar.copy(a_sb[0][:], a_ps[0][:])
        nc.vector.tensor_copy(a_sb[1][:], a_ps[1][:])
        weigh(0)
        nc.scalar.copy(a_sb[2][:], a_ps[2][:])
        nc.scalar.copy(a_sb[3][:], a_ps[3][:])
        for t in (2, 3, 1):
            weigh(t)

        og_w, og_s = gather_packed(xo_w, xo_plane, idx2, J, U16, "og")
        b_ps = [ps.tile([P, 2, J], F32, name="b_ps%d" % u) for u in range(2)]
        for t in range(PACK):
            first_stage(b_ps[t // 2][:, t % 2, :], t, og_w, og_s, E2M1)

        y_ps = [ps.tile([P, O], F32, name="y_ps%d" % m) for m in range(2)]
        for m in range(2):
            nc.tensor.matmul_mx(
                out=y_ps[m][:], lhsT=ws_w[:, m * P : (m + 1) * P].bitcast(E5M2),
                lhsT_scale=out_planes[:, m * P : (m + 1) * P],
                rhs=x7_w[:].bitcast(E4M3), rhs_scale=x7_s[:], start=True, stop=False,
            )

        board = [tile([P, C], F32, "board%d" % t) for t in range(PACK)]
        for t in range(PACK):
            (nc.gpsimd if t < 2 else nc.vector).memset(board[t][:], 0.0)
        for t in (0, 2, 1):
            nc.vector.tensor_copy(board[t][:].indirect(idx4[:]), h1[t][:])
        nc.scalar.activation(board[3][:].indirect(idx4[:]), h1[3][:], COPY)

        b_sb = [tile([P, J], F32, "b_sb%d" % t) for t in range(PACK)]
        for t in range(PACK):
            nc.scalar.copy(b_sb[t][:], b_ps[t // 2][:, t % 2, :])

        pg = tile([P, PACK, O], F32, "pg")
        bg = tile([P, PACK, O], F32, "bg")
        for t in (0, 2, 1, 3):
            nc.vector.tensor_copy(pg[:, t, :], board[t][:].indirect(idx5[:]))
        for t in range(PACK):
            nc.scalar.activation(bg[:, t, :], b_sb[t][:].indirect(idx6[:]), COPY)

        hid = tile([P, O, PACK], BF16, "hid")
        hid_w = tile([P, O], U32, "hid_w")
        hid_s = tile([P, O], U8, "hid_s")
        halves = [slice(0, O // 2), slice(O // 2, O)]
        for h in halves:
            nc.vector.tensor_tensor(
                hid[:, h, :].rearrange("p (c i) t -> p c t i", i=4),
                pg[:, :, h].rearrange("p t (c i) -> p c t i", i=4),
                bg[:, :, h].rearrange("p t (c i) -> p c t i", i=4),
                MAX,
            )
        for h in halves:
            nc.vector.quantize_mx(
                out=hid_w[:, h].bitcast(E4M3), scales=hid_s[:, h], in_=hid[:, h, :].rearrange("p o t -> p (o t)")
            )

        y_sb = [tile([P, O], F32, "y_sb%d" % m) for m in range(2)]
        for m in range(2):
            nc.tensor.matmul_mx(
                out=y_ps[m][:], lhsT=wb_w[:, m * P : (m + 1) * P].bitcast(E5M2),
                lhsT_scale=out_planes[:, N + m * P : N + (m + 1) * P],
                rhs=hid_w[:].bitcast(E4M3), rhs_scale=hid_s[:], start=False, stop=True,
            )
        nc.scalar.copy(y_sb[0][:], y_ps[0][:])
        nc.scalar.dma_start(out[0:P, :], y_sb[0][:])
        nc.vector.tensor_copy(y_sb[1][:], y_ps[1][:])
        nc.sync.dma_start(out[P : 2 * P, :], y_sb[1][:])
